import numpy as np
import ml_dtypes


def mxq(x, axis, fmt="e4m3"):
    dtype, down = {"e4m3": (ml_dtypes.float8_e4m3fn, 7), "e5m2": (ml_dtypes.float8_e5m2, 14)}[fmt]
    v = np.moveaxis(np.asarray(x, np.float32).astype(ml_dtypes.bfloat16).astype(np.float64), axis, -1)
    blocks = v.reshape(v.shape[:-1] + (-1, 32))
    amax = np.abs(blocks).max(-1, keepdims=True)
    byte = np.maximum(np.where(amax > 0, np.frexp(amax)[1] - 1 + 127, 0) - down, 1)
    scale = np.exp2(byte - 127.0)
    codes = (blocks / scale).astype(np.float32).astype(dtype).astype(np.float64)
    return np.moveaxis((codes * scale).reshape(v.shape), -1, axis)


WIDE = False


def mx_kscale(k):
    if not WIDE:
        return np.ones(k)
    levels = np.array([10, -10, 5, -5, 0])
    if k % 512:
        return np.exp2(np.random.permutation(np.resize(levels, k // 32))).repeat(32)
    a = np.empty((k // 512, 16))
    for p in range(k // 512):
        a[p, :8] = np.random.permutation(np.resize(levels, 8))
        for g in range(8):
            far = levels[np.abs(levels - a[p, g]) >= 10]
            a[p, g + 8] = far[np.random.randint(len(far))]
    return np.exp2(a.ravel()).repeat(32)


BF16 = ml_dtypes.bfloat16


def bf(x):
    return np.asarray(x, np.float32).astype(BF16)


def f64(x):
    return np.asarray(x).astype(np.float64)


P, T, K, N, J = 4, 1024, 512, 512, 256


def sigmoid(a):
    return 1.0 / (1.0 + np.exp(-a))


def softplus(a):
    return np.maximum(a, 0.0) + np.log(1.0 + np.exp(-np.abs(a)))


def draw0():
    s, u = mx_kscale(K), mx_kscale(T)
    return {"x": bf(np.random.standard_normal((P, T, K)) * s),
            "w_value": bf(2.0 * np.random.standard_normal((K, N)) / np.sqrt(K) / s[:, None]),
            "w_gate": bf(np.random.standard_normal((K, N)) / np.sqrt(K) / s[:, None]),
            "gate_bias": bf(0.5 * np.random.standard_normal(N)),
            "severity": bf(np.exp(0.3 * np.random.standard_normal((P, T))) * u),
            "reliability": bf((0.5 + np.random.random_sample((P, T))) / u),
            "age": bf(np.random.uniform(0.02, 1.0, (P, T))),
            "rate": bf(np.exp(np.random.uniform(np.log(0.25), np.log(3.0), J))),
            "amp": bf(1.0 + 0.1 * np.random.standard_normal(J)),
            "base": bf(0.3 * np.random.standard_normal(N)),
            "mix": bf((0.5 + np.random.random_sample(J)) / J)}


def core(x, w_value, w_gate, gate_bias, severity, reliability, age, rate, amp, base, mix):
    xq = mxq(f64(x).reshape(P * T, K), 1, "e4m3")
    value = xq @ mxq(f64(w_value), 0, "e4m3")
    gate = xq @ mxq(f64(w_gate), 0, "e4m3")
    event = value * sigmoid(gate + f64(gate_bias)) * f64(severity).reshape(P * T, 1)
    event = event.reshape(P, T, N)
    decay = np.exp(-f64(rate)[None, :, None] * f64(age)[:, None, :])
    weight = decay * f64(reliability)[:, None, :]
    pooled = mxq(weight, 2, "e4m3") @ mxq(event, 1, "e4m3")
    size = np.sqrt((decay * decay).sum(axis=2))
    score = pooled * (f64(amp)[None, :] / size)[:, :, None] + f64(base)
    hazard = (softplus(score) * f64(mix)[None, :, None]).sum(axis=1)
    risk = 1.0 - np.exp(-hazard)
    return score, risk


def e4m3fn_bytes(y):
    return np.clip(np.asarray(y, np.float64), -448.0, 448.0).astype(np.float32).astype(ml_dtypes.float8_e4m3fn).view(np.uint8)


def e4m3fn_values(b):
    return np.asarray(b, np.uint8).view(ml_dtypes.float8_e4m3fn).astype(np.float64)


def setup_inputs():
    d = draw0()
    x0 = np.asarray(d['x']).astype(np.float64)
    s = (np.max(np.abs(x0), axis=(0, 1), keepdims=True) / 448.0).astype(np.float32)
    out = {}
    for k, v in d.items():
        if k == 'x':
            out['x_bytes'] = e4m3fn_bytes(x0 / s.astype(np.float64))
            out['x_scale'] = s
        else:
            out[k] = v
    return out


def reference(x_bytes, x_scale, w_value, w_gate, gate_bias, severity, reliability, age, rate, amp, base, mix):
    return core(e4m3fn_values(x_bytes) * x_scale.astype(np.float64), w_value, w_gate, gate_bias, severity, reliability, age, rate, amp, base, mix)

@@ -1,0 +1,509 @@
+from contextlib import ExitStack
+
+import concourse.mybir as mybir
+from concourse.masks import make_identity
+
+PATIENTS, EVENTS, FEATURES, OUTCOMES, RATES = 4, 1024, 512, 512, 256
+FLOPS = 2 * PATIENTS * EVENTS * FEATURES * OUTCOMES * 2 + 2 * PATIENTS * RATES * EVENTS * OUTCOMES
+
+P = 128
+F32 = mybir.dt.float32
+BF16 = mybir.dt.bfloat16
+U32 = mybir.dt.uint32
+U8 = mybir.dt.uint8
+E4M3 = mybir.dt.float8_e4m3fn
+E4M3X4 = mybir.dt.float8_e4m3fn_x4
+ALU = mybir.AluOpType
+ACT = mybir.ActivationFunctionType
+AX = mybir.AxisListType
+
+GROUPS = PATIENTS * EVENTS // 512
+SOFTPLUS_CAP = 30.0
+PIECES = (1, 1, 1, 2)
+V_WIDEN = 1
+XW_BUFS = 4
+LAG = 3
+LEAD = 11
+LEAD0 = 13
+HEADX = 0
+VLEAD = 4
+PO0 = 1
+PO1 = 2
+SPE = 4
+XNUM = 4
+XDEN = 2
+MLN = 99
+MLP = 0
+V_EVAC = (5, 9, 17, 18, 20, 24,)
+ORDER = ("evq", "event", "x", "gate", "pool", "extra", "value", "widen",)
+
+
+def tile_decayed_event_risk_f4_kernel(
+    tc, x_bytes, x_scale, w_value, w_gate, gate_bias, severity, reliability, age, rate, amp, base, mix, score, risk
+):
+    nc = tc.nc
+    with ExitStack() as ctx:
+        const = ctx.enter_context(tc.tile_pool(name="const", bufs=1))
+        work = ctx.enter_context(tc.tile_pool(name="work", bufs=2))
+        psum = ctx.enter_context(tc.psum_pool(name="psum", bufs=2))
+        ctx.enter_context(tc.manual_schedule())
+
+        def bank(tag, name, shape, dtype=F32):
+            return psum.tile(shape, dtype, name=name, tag=tag, bufs=2)
+
+        rows = const.tile([P, 512], BF16, name="rows")
+        prows = const.tile([P, P], BF16, name="prows")
+        val = const.tile([P, RATES], BF16, name="val")
+        nc.vector.memset(rows[:], 0.0)
+        nc.vector.memset(prows[:], 0.0)
+        nc.vector.memset(val[:], 1.0)
+        warm = const.tile([P, 1], F32, name="warm")
+        nc.vector.memset(warm[:], 1.0)
+
+        x_view = x_bytes.rearrange("i (g p t) k -> (i g) p (t k)", g=2, p=P, t=4)
+        xb = []
+        for g in range(GROUPS):
+            xb_g = const.tile([P, 2048], U8, name="xb%d" % g, align_bytes=64)
+            xb.append(xb_g)
+        age_b = const.tile([P, PATIENTS, EVENTS], BF16, name="age_b")
+        w_raw = {}
+        for key in ("g", "v"):
+            raw = const.tile([P, 4, OUTCOMES], BF16, name="w_raw_" + key)
+            w_raw[key] = raw
+        xs_col = const.tile([P, 4], F32, name="xs_col")
+        base_b = const.tile([P, OUTCOMES], BF16, name="base_b")
+        nc.scalar.dma_start(out=rows[8:16, :], in_=reliability.rearrange("i (g q) -> (i g) q", g=2))
+        nc.scalar.dma_start(out=rows[0:8, :], in_=age.rearrange("i (g q) -> (i g) q", g=2))
+        nc.scalar.dma_start(out=prows[0:2, :], in_=rate.rearrange("(a b) -> a b", b=P))
+        nc.scalar.dma_start(out=rows[16:24, :], in_=severity.rearrange("i (g q) -> (i g) q", g=2))
+        nc.scalar.dma_start(out=prows[2:4, :], in_=amp.rearrange("(a b) -> a b", b=P))
+        nc.scalar.dma_start(out=prows[4:6, :], in_=mix.rearrange("(a b) -> a b", b=P))
+        nc.scalar.dma_start(out=prows[6:10, :], in_=gate_bias.rearrange("(a b) -> a b", b=P))
+        nc.scalar.dma_start(out=val[0:32, :], in_=rate.partition_broadcast(32))
+
+        def load_x(g):
+            nc.sync.dma_start(out=xb[g][:], in_=x_view[g])
+
+        def load_age(i):
+            nc.sync.dma_start(out=age_b[:, i, :], in_=age[i].partition_broadcast(P))
+
+        load_x(0)
+        nc.sync.dma_start(out=xs_col[:], in_=x_scale.rearrange("a b (p f) -> (a b p) f", f=4))
+        load_age(0)
+        nc.sync.dma_start(out=w_raw["v"][:], in_=w_value.rearrange("(p j) n -> p j n", j=4))
+        nc.sync.dma_start(out=w_raw["g"][:], in_=w_gate.rearrange("(p j) n -> p j n", j=4))
+        load_x(1)
+        load_x(2)
+        load_age(1)
+        load_x(3)
+        load_x(4)
+        load_age(2)
+        load_x(5)
+        load_age(3)
+        nc.sync.dma_start(out=base_b[:], in_=base.partition_broadcast(P))
+        load_x(6)
+        load_x(7)
+
+        nc.scalar.activation(out=warm[:], in_=warm[:], func=ACT.Ln)
+        ident_b = const.tile([P, P], BF16, name="ident_b")
+        make_identity(nc, ident_b[:])
+        ident_f = const.tile([P, P], F32, name="ident_f")
+        make_identity(nc, ident_f[:])
+        neg_half = const.tile([P, 2], F32, name="neg_half")
+        nc.gpsimd.memset(neg_half[:], -0.5)
+
+        cols_ps = bank("m", "cols_ps", [P, 4, P], BF16)
+        for t in range(4):
+            nc.tensor.transpose(cols_ps[:, t, :], rows[:, t : 512 : 4], ident_b[:])
+        cols = const.tile([P, 24, 4], F32, name="cols")
+        nc.vector.tensor_copy(out=cols[:], in_=cols_ps[:, :, 0:24].rearrange("p t c -> p c t"))
+        prm_ps = bank("m", "prm_ps", [P, P], BF16)
+        nc.tensor.transpose(prm_ps[:], prows[:], ident_b[:])
+        prm = const.tile([P, 10], F32, name="prm")
+        nc.vector.tensor_copy(out=prm[:], in_=prm_ps[:, 0:10])
+        rate_m2 = const.tile([P, 2], F32, name="rate_m2")
+        nc.vector.tensor_scalar(out=rate_m2[:], in0=prm[:, 0:2], scalar1=-2.0, scalar2=None, op0=ALU.mult)
+        rel_c = cols[:, 8:16, :].rearrange("p c t -> p (c t)")
+        l0 = const.tile([P, 32], F32, name="l0")
+        inv = const.tile([P, 32], F32, name="inv")
+        nc.scalar.activation(out=l0[:], in_=rel_c, func=ACT.Ln)
+        nc.scalar.activation(out=inv[:], in_=l0[:], func=ACT.Exp, scale=-1.0)
+        sev_half = const.tile([P, 32], F32, name="sev_half")
+        bias_half = const.tile([P, 4], F32, name="bias_half")
+        mask_t = const.tile([P, 4], F32, name="mask_t")
+        mask_g = const.tile([P, GROUPS], F32, name="mask_g")
+        lnrel = const.tile([P, 32], F32, name="lnrel")
+        parts = const.tile([P, 4, 32], BF16, name="parts")
+        parts_t = const.tile([P, P], BF16, name="parts_t")
+        arg_rhs = const.tile([P, 2, 4, P], BF16, name="arg_rhs")
+        arg_lhs = []
+
+        def tables_a():
+            nc.vector.tensor_scalar(
+                out=sev_half[:], in0=cols[:, 16:24, :].rearrange("p c t -> p (c t)"),
+                scalar1=0.5, scalar2=None, op0=ALU.mult,
+            )
+            nc.vector.tensor_scalar(out=bias_half[:], in0=prm[:, 6:10], scalar1=0.5, scalar2=None, op0=ALU.mult)
+            nc.vector.tensor_reduce(
+                out=mask_t[:], in_=ident_f[:].rearrange("p (q t) -> p t q", t=4), axis=AX.X, op=ALU.add
+            )
+            nc.vector.tensor_reduce(
+                out=mask_g[:], in_=ident_f[:].rearrange("p (s g t) -> p g s t", s=4, t=4), axis=AX.XY, op=ALU.add
+            )
+            nc.vector.tensor_scalar(
+                out=mask_t[0:32, :], in0=mask_t[0:32, :], scalar1=-1.0, scalar2=None, op0=ALU.mult
+            )
+            nc.vector.tensor_copy(out=parts[:, 0, :], in_=cols[:, 0:8, :].rearrange("p c t -> p (c t)"))
+            nc.vector.tensor_tensor(out=lnrel[:], in0=inv[:], in1=rel_c, op=ALU.mult)
+            nc.vector.scalar_tensor_tensor(
+                out=lnrel[:], in0=lnrel[:], scalar=-1.0, in1=l0[:], op0=ALU.add, op1=ALU.add
+            )
+            for s in (1, 2, 3):
+                nc.vector.tensor_copy(out=parts[:, s, :], in_=lnrel[:])
+                if s < 3:
+                    nc.vector.tensor_tensor(out=lnrel[:], in0=lnrel[:], in1=parts[:, s, :], op=ALU.subtract)
+            parts_ps = bank("m", "parts_ps", [P, P], BF16)
+            nc.tensor.transpose(parts_ps[:], parts[:].rearrange("p s c -> p (s c)"), ident_b[:])
+            nc.vector.tensor_copy(out=parts_t[:], in_=parts_ps[:])
+
+        def tables_c():
+            for t in range(4):
+                nc.vector.tensor_scalar(
+                    out=arg_rhs[:, :, t, :], in0=val[:].rearrange("p (a j) -> p a j", j=P),
+                    scalar1=mask_t[:, t : t + 1], scalar2=None, op0=ALU.mult,
+                )
+
+        def tables_b(groups):
+            for g in groups:
+                lhs_g = const.tile([P, P], BF16, name="arg_lhs%d" % g)
+                nc.vector.tensor_scalar(
+                    out=lhs_g[:], in0=parts_t[:], scalar1=mask_g[:, g : g + 1], scalar2=None, op0=ALU.mult
+                )
+                arg_lhs.append(lhs_g)
+
+        w_codes, w_scales = {}, {}
+
+        def weights_copy(key, engine):
+            grouped = work.tile([P, OUTCOMES, 4], BF16, name="w_grouped_" + key, tag="w_grouped", bufs=2, align_bytes=64)
+            w_codes[key] = grouped
+            if engine == "v":
+                nc.vector.tensor_copy(out=grouped[:], in_=w_raw[key][:].rearrange("p j n -> p n j"))
+            else:
+                nc.scalar.copy(out=grouped[:], in_=w_raw[key][:].rearrange("p j n -> p n j"))
+
+        def weights_quant(key):
+            grouped = w_codes[key]
+            codes = const.tile([P, OUTCOMES], U32, name="w_codes_" + key, align_bytes=64)
+            scales = const.tile([P, OUTCOMES], U8, name="w_scales_" + key, align_bytes=64)
+            nc.vector.quantize_mx(
+                out=codes[:].bitcast(E4M3X4), scales=scales[:], in_=grouped[:].rearrange("p n j -> p (n j)")
+            )
+            w_codes[key], w_scales[key] = codes, scales
+
+        xw, xi, x_codes, x_scales = {}, {}, {}, {}
+
+        def x_widen(g, t):
+            if t == 0:
+                xw[g] = work.tile([P, 2048], BF16, name="xw%d" % g, tag="xw", bufs=XW_BUFS)
+            c = slice(FEATURES * t, FEATURES * (t + 1))
+            engine = nc.vector if g < V_WIDEN else nc.gpsimd
+            engine.tensor_copy(out=xw[g][:, c], in_=xb[g][:, c].bitcast(E4M3))
+
+        def x_turn(g, h):
+            if h == 0:
+                xi[g] = work.tile([P, 512, 4], BF16, name="xi%d" % g, tag="xi", bufs=2, align_bytes=64)
+            words = xw[g][:].bitcast(F32)
+            turned = bank("m", "xt%d_%d" % (g, h), [P, 2, 2, P])
+            for t in range(2):
+                for u in range(2):
+                    c0 = 256 * (2 * h + t)
+                    nc.tensor.transpose(turned[:, u, t, :], words[:, c0 + u : c0 + 256 : 2], ident_f[:])
+            pairs = turned[:].rearrange("p u t r -> p (u t r)").bitcast(BF16)
+            nc.vector.tensor_tensor(
+                out=xi[g][:, 256 * h : 256 * (h + 1), :].rearrange("p n (u e) -> p n u e", u=2),
+                in0=pairs.rearrange("p (u n e) -> p n u e", u=2, e=2),
+                in1=xs_col[:].rearrange("p (o u e) -> p o u e", o=1, u=2).to_broadcast([P, 256, 2, 2]),
+                op=ALU.mult,
+            )
+
+        def x_quant(g):
+            codes = const.tile([P, 512], U32, name="x_codes%d" % g, align_bytes=64)
+            scales = const.tile([P, 512], U8, name="x_scales%d" % g, align_bytes=64)
+            nc.vector.quantize_mx(
+                out=codes[:].bitcast(E4M3X4), scales=scales[:], in_=xi[g][:].rearrange("p n f -> p (n f)")
+            )
+            x_codes[g], x_scales[g] = codes, scales
+
+        sum_sq = const.tile([P, PATIENTS, 2], F32, name="sum_sq")
+        amp_over_size = const.tile([P, PATIENTS, 2], F32, name="amp_over_size")
+
+        def size(i, a):
+            junk = work.tile([P, EVENTS], BF16, name="junk%d_%d" % (i, a), tag="junk", bufs=2)
+            nc.scalar.activation(
+                out=junk[:], in_=age_b[:, i, :], func=ACT.Exp, scale=rate_m2[:, a : a + 1],
+                accum_out=sum_sq[:, i, a : a + 1],
+            )
+            if a == 1:
+                nc.gpsimd.tensor_tensor(out=amp_over_size[:, i, :], in0=sum_sq[:, i, :], in1=neg_half[:], op=ALU.pow)
+                nc.gpsimd.tensor_tensor(
+                    out=amp_over_size[:, i, :], in0=amp_over_size[:, i, :], in1=prm[:, 2:4], op=ALU.mult
+                )
+
+        wt, wt_codes, wt_scales = {}, {}, {}
+
+        def weight_exp(g, a):
+            if a == 0:
+                wt[g] = work.tile([P, RATES, 4], BF16, name="wt%d" % g, tag="wt", bufs=4, align_bytes=64)
+            arg = bank("m", "arg%d_%d" % (g, a), [P, 4, P])
+            nc.tensor.matmul(
+                arg[:].rearrange("p t j -> p (t j)"), lhsT=arg_lhs[g][:],
+                rhs=arg_rhs[:, a].rearrange("p t j -> p (t j)"), start=True, stop=True,
+            )
+            nc.scalar.activation(
+                out=wt[g][:, P * a : P * (a + 1), :], in_=arg[:].rearrange("p t j -> p j t"), func=ACT.Exp
+            )
+
+        def weight_quant(g):
+            codes = const.tile([P, RATES], U32, name="wt_codes%d" % g, align_bytes=64)
+            scales = const.tile([P, RATES], U8, name="wt_scales%d" % g, align_bytes=64)
+            nc.vector.quantize_mx(
+                out=codes[:].bitcast(E4M3X4), scales=scales[:], in_=wt[g][:].rearrange("p j t -> p (j t)")
+            )
+            wt_codes[g], wt_scales[g] = codes, scales
+
+        val_sb, th, ev, ev_codes, ev_scales = {}, {}, {}, {}, {}
+
+        def value(g, t, engine):
+            if t == 0:
+                val_sb[g] = work.tile([P, 4, OUTCOMES], F32, name="val_sb%d" % g, tag="val_sb", bufs=2)
+            c = slice(P * t, P * (t + 1))
+            vb = bank("val", "val%d_%d" % (g, t), [P, OUTCOMES])
+            nc.tensor.matmul_mx(
+                out=vb[:], lhsT=x_codes[g][:, c].bitcast(E4M3X4), lhsT_scale=x_scales[g][:, c],
+                rhs=w_codes["v"][:].bitcast(E4M3X4), rhs_scale=w_scales["v"][:], start=True, stop=True,
+            )
+            sev = sev_half[:, 4 * g + t : 4 * g + t + 1]
+            if engine == "s":
+                nc.scalar.activation(out=val_sb[g][:, t, :], in_=vb[:], func=ACT.Copy, scale=sev)
+            else:
+                nc.vector.tensor_scalar(out=val_sb[g][:, t, :], in0=vb[:], scalar1=sev, scalar2=None, op0=ALU.mult)
+
+        def gate(g, q):
+            n = slice(P * q, P * (q + 1))
+            gb = bank("gate", "gate%d_%d" % (g, q), [P, 512])
+            nc.tensor.matmul_mx(
+                out=gb[:], lhsT=w_codes["g"][:, n].bitcast(E4M3X4), lhsT_scale=w_scales["g"][:, n],
+                rhs=x_codes[g][:].bitcast(E4M3X4), rhs_scale=x_scales[g][:], start=True, stop=True,
+            )
+            th[g, q] = work.tile([P, 512], F32, name="th%d_%d" % (g, q), tag="th", bufs=4)
+            nc.scalar.activation(out=th[g, q][:], in_=gb[:], func=ACT.Tanh, scale=0.5, bias=bias_half[:, q : q + 1])
+
+        def event(g, q):
+            if q == 0:
+                ev[g] = work.tile([P, OUTCOMES, 4], BF16, name="ev%d" % g, tag="ev", bufs=2, align_bytes=64)
+            n = slice(P * q, P * (q + 1))
+            tt = bank("tt", "tt%d_%d" % (g, q), [P, 4, P])
+            for t in range(4):
+                nc.tensor.transpose(tt[:, t, :], th[g, q][:, P * t : P * (t + 1)], ident_f[:])
+            nc.vector.scalar_tensor_tensor(
+                out=ev[g][:, n, :], in0=tt[:].rearrange("p t n -> p n t"), scalar=1.0,
+                in1=val_sb[g][:, :, n].rearrange("p t n -> p n t"), op0=ALU.add, op1=ALU.mult,
+            )
+
+        def event_quant(g, c0, c1):
+            if c0 == 0:
+                ev_codes[g] = work.tile(
+                    [P, OUTCOMES], U32, name="ev_codes%d" % g, tag="ev_codes", bufs=4, align_bytes=64
+                )
+                ev_scales[g] = work.tile(
+                    [P, OUTCOMES], U8, name="ev_scales%d" % g, tag="ev_scales", bufs=4, align_bytes=64
+                )
+            nc.vector.quantize_mx(
+                out=ev_codes[g][:, c0:c1].bitcast(E4M3X4), scales=ev_scales[g][:, c0:c1],
+                in_=ev[g][:, c0:c1, :].rearrange("p n t -> p (n t)"),
+            )
+
+        sc, sp, haz = {}, {}, {}
+        haz_sb = const.tile([P, P], F32, name="haz_sb")
+        nc.gpsimd.memset(haz_sb[:], 0.0)
+        for i in range(PATIENTS):
+            shape = [P, PIECES[i], 2, OUTCOMES // PIECES[i]]
+            sc[i] = const.tile(shape, F32, name="sc%d" % i)
+            sp[i] = const.tile(shape, F32, name="sp%d" % i)
+
+        def pooled(i, h, a):
+            width = OUTCOMES // PIECES[i]
+            j = slice(P * a, P * (a + 1))
+            n = slice(width * h, width * (h + 1))
+            pb = bank("m", "pool%d_%d_%d" % (i, a, h), [P, width])
+            for k in range(2):
+                g = 2 * i + k
+                nc.tensor.matmul_mx(
+                    out=pb[:], lhsT=wt_codes[g][:, j].bitcast(E4M3X4), lhsT_scale=wt_scales[g][:, j],
+                    rhs=ev_codes[g][:, n].bitcast(E4M3X4), rhs_scale=ev_scales[g][:, n],
+                    start=(k == 0), stop=(k == 1),
+                )
+            nc.vector.scalar_tensor_tensor(
+                out=sc[i][:, h, a, :], in0=pb[:], scalar=amp_over_size[:, i, a : a + 1],
+                in1=base_b[:, n], op0=ALU.mult, op1=ALU.add,
+            )
+            nc.sync.dma_start(out=score[i, j, n], in_=sc[i][:, h, a, :])
+
+        def sp_min(i, h):
+            nc.vector.tensor_scalar(
+                out=sp[i][:, h], in0=sc[i][:, h], scalar1=SOFTPLUS_CAP, scalar2=None, op0=ALU.min
+            )
+
+        def sp_exp(i, h):
+            nc.scalar.activation(out=sp[i][:, h], in_=sp[i][:, h], func=ACT.Exp)
+
+        def sp_ln(i, h):
+            nc.scalar.activation(out=sp[i][:, h], in_=sp[i][:, h], func=ACT.Ln, bias=1.0)
+
+        def sp_sum(i, h):
+            nc.vector.tensor_tensor(out=sp[i][:, h], in0=sp[i][:, h], in1=sc[i][:, h], op=ALU.max)
+            blocks = 4 // PIECES[i]
+            haz[i, h] = bank("m", "haz%d_%d" % (i, h), [P, blocks])
+            for b in range(blocks):
+                for a in range(2):
+                    nc.tensor.matmul(
+                        haz[i, h][:, b : b + 1], lhsT=sp[i][:, h, a, P * b : P * (b + 1)],
+                        rhs=prm[:, 4 + a : 5 + a], start=(a == 0), stop=(a == 1),
+                    )
+
+        def sp_keep(i, h):
+            blocks = 4 // PIECES[i]
+            b0 = 4 * i + blocks * h
+            nc.vector.tensor_copy(out=haz_sb[:, b0 : b0 + blocks], in_=haz[i, h][:])
+
+        for t in range(4):
+            x_widen(0, t)
+        x_turn(0, 0)
+        x_turn(0, 1)
+        x_quant(0)
+        weights_copy("v", "v")
+        tables_a()
+        weights_quant("v")
+        extras = []
+        for i in range(PATIENTS):
+            extras += [("size", i, 0), ("size", i, 1)]
+            for g in (2 * i, 2 * i + 1):
+                extras += [("exp", g, 0), ("exp", g, 1)]
+        extras = extras[::-1]
+        pending = []
+
+        def extra():
+            if extras:
+                kind, g, a = extras.pop()
+                if kind == "size":
+                    size(g, a)
+                    tables_b((2 * g + a,))
+                else:
+                    weight_exp(g, a)
+                    if a == 1:
+                        pending.append(g)
+
+        def widen_piece(w):
+            if 4 <= w < 4 * GROUPS:
+                x_widen(w // 4, w % 4)
+
+        def x_piece(w):
+            if w % 2 == 0 and 4 < w <= 4 * GROUPS:
+                x_turn((w - 1) // 4, (w - 1) % 4 // 2)
+            if w % 4 == 1 and 5 < w <= 4 * GROUPS + 1:
+                x_quant(w // 4 - 1)
+
+        units = [(g, q) for g in range(GROUPS) for q in range(4)]
+
+        def value_piece(v):
+            if v < len(units):
+                value(*units[v], "v" if v in V_EVAC else "s")
+
+        for w in range(4, LEAD0):
+            widen_piece(w)
+        for k in range(2):
+            extra()
+        weights_copy("g", "s")
+        tables_c()
+        weights_quant("g")
+        for k in range(HEADX):
+            extra()
+        vdone = 0
+        for w in range(5, LEAD):
+            x_piece(w)
+            if w - 5 < VLEAD:
+                value_piece(vdone)
+                vdone += 1
+        while vdone < VLEAD:
+            value_piece(vdone)
+            vdone += 1
+        for k in range(LAG):
+            gate(*units[k])
+        hx = 0
+        for s in range(len(units)):
+            g, q = units[s]
+            for item in ORDER:
+                if item == "gate" and s + LAG < len(units):
+                    gate(*units[s + LAG])
+                if item == "widen":
+                    widen_piece(s + LEAD0)
+                if item == "x":
+                    x_piece(s + LEAD)
+                if item == "evq" and s >= 4 and s % 4 == 0:
+                    event_quant(s // 4 - 1, 0, OUTCOMES)
+                if item == "value":
+                    value_piece(s + VLEAD)
+                if item == "event":
+                    event(g, q)
+                if item == "pool" and s >= 8:
+                    i = s // 8 - 1
+                    if s % 8 == PO0:
+                        pooled(i, 0, 0)
+                    if s % 8 == PO1:
+                        pooled(i, 0, 1)
+                        sp_min(i, 0)
+                    if s % 8 == SPE:
+                        sp_exp(i, 0)
+                if item == "extra":
+                    while pending and s % 2 == 1:
+                        weight_quant(pending.pop(0))
+                    if (s * XNUM) // XDEN > hx:
+                        hx += 1
+                        extra()
+            if s == len(units) - 2:
+                event_quant(g, 0, OUTCOMES // 2)
+            if s == MLN:
+                for i in range(MLP):
+                    sp_ln(i, 0)
+                nc.scalar.activation(out=warm[:], in_=warm[:], func=ACT.Exp)
+                for i in range(MLP):
+                    sp_sum(i, 0)
+                    sp_keep(i, 0)
+        while extras:
+            extra()
+        while pending:
+            weight_quant(pending.pop(0))
+        last = PATIENTS - 1
+        event_quant(GROUPS - 1, OUTCOMES // 2, OUTCOMES)
+        for h in range(PIECES[last]):
+            for a in range(2):
+                pooled(last, h, a)
+            sp_min(last, h)
+            sp_exp(last, h)
+        todo = [(i, h) for i in range(MLP, PATIENTS) for h in range(PIECES[i])]
+        for i, h in todo:
+            sp_ln(i, h)
+        for k, (i, h) in enumerate(todo):
+            sp_sum(i, h)
+            if k > 0:
+                sp_keep(*todo[k - 1])
+        sp_keep(*todo[-1])
+        nc.scalar.activation(out=warm[:], in_=warm[:], func=ACT.Exp)
+        turned = bank("m", "haz_t", [P, P])
+        nc.tensor.transpose(turned[:], haz_sb[:], ident_f[:])
+        risk_sb = const.tile([4 * PATIENTS, P], F32, name="risk_sb")
+        nc.scalar.activation(out=risk_sb[:], in_=turned[0 : 4 * PATIENTS, :], func=ACT.Exp, scale=-1.0)
+        nc.vector.tensor_scalar(
+            out=risk_sb[:], in0=risk_sb[:], scalar1=-1.0, scalar2=1.0, op0=ALU.mult, op1=ALU.add
+        )
+        nc.sync.dma_start(out=risk.rearrange("i (b q) -> (i b) q", q=P), in_=risk_sb[:])

@@ -20,22 +20,25 @@ AX = mybir.AxisListType
 GROUPS = PATIENTS * EVENTS // 512
 SOFTPLUS_CAP = 30.0
 PIECES = (1, 1, 1, 2)
-V_WIDEN = 1
-XW_BUFS = 4
-LAG = 3
+HALF = OUTCOMES // 2
+XW_BUFS = 5
+LAG = 2
 LEAD = 11
-LEAD0 = 13
+LEAD0 = 23
 HEADX = 0
 VLEAD = 4
 PO0 = 1
 PO1 = 2
-SPE = 4
+SPE = 7
 XNUM = 4
-XDEN = 2
+XDEN = 4
 MLN = 99
 MLP = 0
-V_EVAC = (5, 9, 17, 18, 20, 24,)
-ORDER = ("evq", "event", "x", "gate", "pool", "extra", "value", "widen",)
+V_EVAC = (5, 9, 17, 18, 24, 29,)
+ORDER = ("gate", "value", "x", "evq", "event", "pool", "widen", "extra",)
+X_MODE = ("v", "g", "g", "g", "g", "g", "g", "g",)
+S_TURN = ()
+COMBINE = (1, 2, 3,)
 
 
 def tile_decayed_event_risk_f4_kernel(
@@ -71,6 +74,7 @@ def tile_decayed_event_risk_f4_kernel(
             raw = const.tile([P, 4, OUTCOMES], BF16, name="w_raw_" + key)
             w_raw[key] = raw
         xs_col = const.tile([P, 4], F32, name="xs_col")
+        xs_row = const.tile([P, FEATURES], F32, name="xs_row")
         base_b = const.tile([P, OUTCOMES], BF16, name="base_b")
         nc.scalar.dma_start(out=rows[8:16, :], in_=reliability.rearrange("i (g q) -> (i g) q", g=2))
         nc.scalar.dma_start(out=rows[0:8, :], in_=age.rearrange("i (g q) -> (i g) q", g=2))
@@ -89,6 +93,8 @@ def tile_decayed_event_risk_f4_kernel(
 
         load_x(0)
         nc.sync.dma_start(out=xs_col[:], in_=x_scale.rearrange("a b (p f) -> (a b p) f", f=4))
+        if "x" in X_MODE:
+            nc.sync.dma_start(out=xs_row[:], in_=x_scale.rearrange("a b k -> (a b k)").partition_broadcast(P))
         load_age(0)
         nc.sync.dma_start(out=w_raw["v"][:], in_=w_value.rearrange("(p j) n -> p j n", j=4))
         nc.sync.dma_start(out=w_raw["g"][:], in_=w_gate.rearrange("(p j) n -> p j n", j=4))
@@ -112,6 +118,9 @@ def tile_decayed_event_risk_f4_kernel(
         neg_half = const.tile([P, 2], F32, name="neg_half")
         nc.gpsimd.memset(neg_half[:], -0.5)
 
+        mix_cols = const.tile([P, 2, PATIENTS * P], F32, name="mix_cols")
+        nc.gpsimd.memset(mix_cols[:], 0.0)
+
         cols_ps = bank("m", "cols_ps", [P, 4, P], BF16)
         for t in range(4):
             nc.tensor.transpose(cols_ps[:, t, :], rows[:, t : 512 : 4], ident_b[:])
@@ -123,6 +132,11 @@ def tile_decayed_event_risk_f4_kernel(
         nc.vector.tensor_copy(out=prm[:], in_=prm_ps[:, 0:10])
         rate_m2 = const.tile([P, 2], F32, name="rate_m2")
         nc.vector.tensor_scalar(out=rate_m2[:], in0=prm[:, 0:2], scalar1=-2.0, scalar2=None, op0=ALU.mult)
+        for a in range(2):
+            nc.gpsimd.tensor_copy(
+                out=mix_cols[:, a, 0 : 3 * P + 4 : P + 1], in_=prm[:, 4 + a : 5 + a].to_broadcast([P, PATIENTS])
+            )
+        mix_ratio = const.tile([P, 1], F32, name="mix_ratio")
         rel_c = cols[:, 8:16, :].rearrange("p c t -> p (c t)")
         l0 = const.tile([P, 32], F32, name="l0")
         inv = const.tile([P, 32], F32, name="inv")
@@ -143,6 +157,9 @@ def tile_decayed_event_risk_f4_kernel(
                 out=sev_half[:], in0=cols[:, 16:24, :].rearrange("p c t -> p (c t)"),
                 scalar1=0.5, scalar2=None, op0=ALU.mult,
             )
+            if COMBINE:
+                nc.vector.reciprocal(out=mix_ratio[:], in_=prm[:, 4:5])
+                nc.vector.tensor_tensor(out=mix_ratio[:], in0=mix_ratio[:], in1=prm[:, 5:6], op=ALU.mult)
             nc.vector.tensor_scalar(out=bias_half[:], in0=prm[:, 6:10], scalar1=0.5, scalar2=None, op0=ALU.mult)
             nc.vector.tensor_reduce(
                 out=mask_t[:], in_=ident_f[:].rearrange("p (q t) -> p t q", t=4), axis=AX.X, op=ALU.add
@@ -206,8 +223,16 @@ def tile_decayed_event_risk_f4_kernel(
             if t == 0:
                 xw[g] = work.tile([P, 2048], BF16, name="xw%d" % g, tag="xw", bufs=XW_BUFS)
             c = slice(FEATURES * t, FEATURES * (t + 1))
-            engine = nc.vector if g < V_WIDEN else nc.gpsimd
-            engine.tensor_copy(out=xw[g][:, c], in_=xb[g][:, c].bitcast(E4M3))
+            src = xb[g][:, c].bitcast(E4M3)
+            mode = X_MODE[g]
+            if mode == "x":
+                nc.vector.tensor_tensor(out=xw[g][:, c], in0=src, in1=xs_row[:], op=ALU.mult)
+            elif mode == "v":
+                nc.vector.tensor_copy(out=xw[g][:, c], in_=src)
+            elif mode == "s":
+                nc.scalar.copy(out=xw[g][:, c], in_=src)
+            else:
+                nc.gpsimd.tensor_copy(out=xw[g][:, c], in_=src)
 
         def x_turn(g, h):
             if h == 0:
@@ -218,6 +243,15 @@ def tile_decayed_event_risk_f4_kernel(
                 for u in range(2):
                     c0 = 256 * (2 * h + t)
                     nc.tensor.transpose(turned[:, u, t, :], words[:, c0 + u : c0 + 256 : 2], ident_f[:])
+            if X_MODE[g] == "x":
+                words_out = xi[g][:].rearrange("p n f -> p (n f)").bitcast(F32)[:, 512 * h : 512 * (h + 1)]
+                words_out = words_out.rearrange("p (n u) -> p n u", u=2)
+                words_in = turned[:].rearrange("p u t r -> p (t r) u")
+                if 2 * g + h in S_TURN:
+                    nc.scalar.copy(out=words_out, in_=words_in)
+                else:
+                    nc.vector.tensor_copy(out=words_out, in_=words_in)
+                return
             pairs = turned[:].rearrange("p u t r -> p (u t r)").bitcast(BF16)
             nc.vector.tensor_tensor(
                 out=xi[g][:, 256 * h : 256 * (h + 1), :].rearrange("p n (u e) -> p n u e", u=2),
@@ -323,9 +357,7 @@ def tile_decayed_event_risk_f4_kernel(
                 in_=ev[g][:, c0:c1, :].rearrange("p n t -> p (n t)"),
             )
 
-        sc, sp, haz = {}, {}, {}
-        haz_sb = const.tile([P, P], F32, name="haz_sb")
-        nc.gpsimd.memset(haz_sb[:], 0.0)
+        sc, sp = {}, {}
         for i in range(PATIENTS):
             shape = [P, PIECES[i], 2, OUTCOMES // PIECES[i]]
             sc[i] = const.tile(shape, F32, name="sc%d" % i)
@@ -360,21 +392,29 @@ def tile_decayed_event_risk_f4_kernel(
         def sp_ln(i, h):
             nc.scalar.activation(out=sp[i][:, h], in_=sp[i][:, h], func=ACT.Ln, bias=1.0)
 
-        def sp_sum(i, h):
+        def sp_max(i, h):
             nc.vector.tensor_tensor(out=sp[i][:, h], in0=sp[i][:, h], in1=sc[i][:, h], op=ALU.max)
-            blocks = 4 // PIECES[i]
-            haz[i, h] = bank("m", "haz%d_%d" % (i, h), [P, blocks])
-            for b in range(blocks):
-                for a in range(2):
-                    nc.tensor.matmul(
-                        haz[i, h][:, b : b + 1], lhsT=sp[i][:, h, a, P * b : P * (b + 1)],
-                        rhs=prm[:, 4 + a : 5 + a], start=(a == 0), stop=(a == 1),
-                    )
+            if i in COMBINE:
+                nc.vector.scalar_tensor_tensor(
+                    out=sp[i][:, h, 0, :], in0=sp[i][:, h, 1, :], scalar=mix_ratio[:, 0:1],
+                    in1=sp[i][:, h, 0, :], op0=ALU.mult, op1=ALU.add,
+                )
 
-        def sp_keep(i, h):
-            blocks = 4 // PIECES[i]
-            b0 = 4 * i + blocks * h
-            nc.vector.tensor_copy(out=haz_sb[:, b0 : b0 + blocks], in_=haz[i, h][:])
+        haz = {}
+
+        def sp_sum(i, h):
+            width = OUTCOMES // PIECES[i]
+            for b in range(2):
+                if PIECES[i] == 2 and b != h:
+                    continue
+                if b not in haz:
+                    haz[b] = bank("m", "haz%d" % b, [P, HALF])
+                n0 = HALF * b - width * h
+                for a in range(1 if i in COMBINE else 2):
+                    nc.tensor.matmul(
+                        haz[b][:], lhsT=mix_cols[:, a, P * i : P * (i + 1)], rhs=sp[i][:, h, a, n0 : n0 + HALF],
+                        start=(i == 0 and a == 0), stop=(i == PATIENTS - 1 and a == (0 if i in COMBINE else 1)),
+                    )
 
         for t in range(4):
             x_widen(0, t)
@@ -477,8 +517,7 @@ def tile_decayed_event_risk_f4_kernel(
                     sp_ln(i, 0)
                 nc.scalar.activation(out=warm[:], in_=warm[:], func=ACT.Exp)
                 for i in range(MLP):
-                    sp_sum(i, 0)
-                    sp_keep(i, 0)
+                    sp_max(i, 0)
         while extras:
             extra()
         while pending:
@@ -493,17 +532,17 @@ def tile_decayed_event_risk_f4_kernel(
         todo = [(i, h) for i in range(MLP, PATIENTS) for h in range(PIECES[i])]
         for i, h in todo:
             sp_ln(i, h)
-        for k, (i, h) in enumerate(todo):
+        for i in range(MLP):
+            sp_sum(i, 0)
+        for i, h in todo:
+            sp_max(i, h)
             sp_sum(i, h)
-            if k > 0:
-                sp_keep(*todo[k - 1])
-        sp_keep(*todo[-1])
         nc.scalar.activation(out=warm[:], in_=warm[:], func=ACT.Exp)
-        turned = bank("m", "haz_t", [P, P])
-        nc.tensor.transpose(turned[:], haz_sb[:], ident_f[:])
-        risk_sb = const.tile([4 * PATIENTS, P], F32, name="risk_sb")
-        nc.scalar.activation(out=risk_sb[:], in_=turned[0 : 4 * PATIENTS, :], func=ACT.Exp, scale=-1.0)
-        nc.vector.tensor_scalar(
-            out=risk_sb[:], in0=risk_sb[:], scalar1=-1.0, scalar2=1.0, op0=ALU.mult, op1=ALU.add
-        )
-        nc.sync.dma_start(out=risk.rearrange("i (b q) -> (i b) q", q=P), in_=risk_sb[:])
+        for b in range(2):
+            n = slice(HALF * b, HALF * (b + 1))
+            risk_sb = const.tile([PATIENTS, HALF], F32, name="risk_sb%d" % b)
+            nc.scalar.activation(out=risk_sb[:], in_=haz[b][0:PATIENTS, :], func=ACT.Exp, scale=-1.0)
+            nc.vector.tensor_scalar(
+                out=risk_sb[:], in0=risk_sb[:], scalar1=-1.0, scalar2=1.0, op0=ALU.mult, op1=ALU.add
+            )
+            nc.sync.dma_start(out=risk[:, n], in_=risk_sb[:])

@@ -21,24 +21,27 @@ GROUPS = PATIENTS * EVENTS // 512
 SOFTPLUS_CAP = 30.0
 PIECES = (1, 1, 1, 2)
 HALF = OUTCOMES // 2
-XW_BUFS = 5
-LAG = 2
-LEAD = 11
-LEAD0 = 23
-HEADX = 0
-VLEAD = 4
-PO0 = 1
+XW_BUFS = 4
+LAG = 3
+LEAD = 12
+LEAD0 = 12
+VLEAD = 6
+PO0 = 0
 PO1 = 2
-SPE = 7
-XNUM = 4
+SPE = 4
+XNUM = 3
 XDEN = 4
 MLN = 99
 MLP = 0
-V_EVAC = (5, 9, 17, 18, 24, 29,)
-ORDER = ("gate", "value", "x", "evq", "event", "pool", "widen", "extra",)
-X_MODE = ("v", "g", "g", "g", "g", "g", "g", "g",)
-S_TURN = ()
+V_EVAC = (5, 7, 9, 13, 16, 18, 23, 25, 27, 30,)
+ORDER = ("extra", "evq", "widen", "event", "x", "gate", "value", "pool",)
+X_MODE = ("v", "x", "x", "x", "x", "x", "x", "x",)
+S_TURN = (4, 6, 7, 8, 9, 10, 11, 12, 13, 14, 15,)
 COMBINE = (1, 2, 3,)
+PL0 = 31
+PL1 = 31
+GATE0 = 8
+HNUM = 3
 
 
 def tile_decayed_event_risk_f4_kernel(
@@ -153,14 +156,31 @@ def tile_decayed_event_risk_f4_kernel(
         arg_lhs = []
 
         def tables_a():
-            nc.vector.tensor_scalar(
+            nc.gpsimd.tensor_scalar(
                 out=sev_half[:], in0=cols[:, 16:24, :].rearrange("p c t -> p (c t)"),
-                scalar1=0.5, scalar2=None, op0=ALU.mult,
+                scalar1=0.5, scalar2=0.0, op0=ALU.mult, op1=ALU.add,
             )
+            nc.gpsimd.tensor_scalar(
+                out=bias_half[:], in0=prm[:, 6:10], scalar1=0.5, scalar2=0.0, op0=ALU.mult, op1=ALU.add
+            )
+            nc.gpsimd.tensor_copy(out=parts[:, 0, :], in_=cols[:, 0:8, :].rearrange("p c t -> p (c t)"))
+            nc.gpsimd.tensor_tensor(out=lnrel[:], in0=inv[:], in1=rel_c, op=ALU.mult)
+            nc.gpsimd.tensor_scalar(
+                out=lnrel[:], in0=lnrel[:], scalar1=-1.0, scalar2=0.0, op0=ALU.add, op1=ALU.add
+            )
+            nc.gpsimd.tensor_tensor(out=lnrel[:], in0=lnrel[:], in1=l0[:], op=ALU.add)
+            for s in (1, 2, 3):
+                nc.gpsimd.tensor_copy(out=parts[:, s, :], in_=lnrel[:])
+                if s < 3:
+                    nc.gpsimd.tensor_tensor(out=lnrel[:], in0=lnrel[:], in1=parts[:, s, :], op=ALU.subtract)
+            parts_ps = bank("m", "parts_ps", [P, P], BF16)
+            nc.tensor.transpose(parts_ps[:], parts[:].rearrange("p s c -> p (s c)"), ident_b[:])
+            return parts_ps
+
+        def tables_b0(parts_ps):
             if COMBINE:
                 nc.vector.reciprocal(out=mix_ratio[:], in_=prm[:, 4:5])
                 nc.vector.tensor_tensor(out=mix_ratio[:], in0=mix_ratio[:], in1=prm[:, 5:6], op=ALU.mult)
-            nc.vector.tensor_scalar(out=bias_half[:], in0=prm[:, 6:10], scalar1=0.5, scalar2=None, op0=ALU.mult)
             nc.vector.tensor_reduce(
                 out=mask_t[:], in_=ident_f[:].rearrange("p (q t) -> p t q", t=4), axis=AX.X, op=ALU.add
             )
@@ -170,17 +190,6 @@ def tile_decayed_event_risk_f4_kernel(
             nc.vector.tensor_scalar(
                 out=mask_t[0:32, :], in0=mask_t[0:32, :], scalar1=-1.0, scalar2=None, op0=ALU.mult
             )
-            nc.vector.tensor_copy(out=parts[:, 0, :], in_=cols[:, 0:8, :].rearrange("p c t -> p (c t)"))
-            nc.vector.tensor_tensor(out=lnrel[:], in0=inv[:], in1=rel_c, op=ALU.mult)
-            nc.vector.scalar_tensor_tensor(
-                out=lnrel[:], in0=lnrel[:], scalar=-1.0, in1=l0[:], op0=ALU.add, op1=ALU.add
-            )
-            for s in (1, 2, 3):
-                nc.vector.tensor_copy(out=parts[:, s, :], in_=lnrel[:])
-                if s < 3:
-                    nc.vector.tensor_tensor(out=lnrel[:], in0=lnrel[:], in1=parts[:, s, :], op=ALU.subtract)
-            parts_ps = bank("m", "parts_ps", [P, P], BF16)
-            nc.tensor.transpose(parts_ps[:], parts[:].rearrange("p s c -> p (s c)"), ident_b[:])
             nc.vector.tensor_copy(out=parts_t[:], in_=parts_ps[:])
 
         def tables_c():
@@ -309,7 +318,7 @@ def tile_decayed_event_risk_f4_kernel(
 
         def value(g, t, engine):
             if t == 0:
-                val_sb[g] = work.tile([P, 4, OUTCOMES], F32, name="val_sb%d" % g, tag="val_sb", bufs=2)
+                val_sb[g] = work.tile([P, 4, OUTCOMES], F32, name="val_sb%d" % g, tag="val_sb", bufs=3)
             c = slice(P * t, P * (t + 1))
             vb = bank("val", "val%d_%d" % (g, t), [P, OUTCOMES])
             nc.tensor.matmul_mx(
@@ -334,7 +343,7 @@ def tile_decayed_event_risk_f4_kernel(
 
         def event(g, q):
             if q == 0:
-                ev[g] = work.tile([P, OUTCOMES, 4], BF16, name="ev%d" % g, tag="ev", bufs=2, align_bytes=64)
+                ev[g] = work.tile([P, OUTCOMES, 4], BF16, name="ev%d" % g, tag="ev", bufs=3, align_bytes=64)
             n = slice(P * q, P * (q + 1))
             tt = bank("tt", "tt%d_%d" % (g, q), [P, 4, P])
             for t in range(4):
@@ -422,8 +431,10 @@ def tile_decayed_event_risk_f4_kernel(
         x_turn(0, 1)
         x_quant(0)
         weights_copy("v", "v")
-        tables_a()
         weights_quant("v")
+        parts_ps = tables_a()
+        tables_b0(parts_ps)
+        tables_c()
         extras = []
         for i in range(PATIENTS):
             extras += [("size", i, 0), ("size", i, 1)]
@@ -453,32 +464,34 @@ def tile_decayed_event_risk_f4_kernel(
             if w % 4 == 1 and 5 < w <= 4 * GROUPS + 1:
                 x_quant(w // 4 - 1)
 
-        units = [(g, q) for g in range(GROUPS) for q in range(4)]
+        units = [(g, q) for g in range(GROUPS - 2) for q in range(4)]
+        units += [(g, 2 * h + k) for h in range(2) for g in (GROUPS - 2, GROUPS - 1) for k in range(2)]
 
         def value_piece(v):
             if v < len(units):
-                value(*units[v], "v" if v in V_EVAC else "s")
+                value(v // 4, v % 4, "v" if v in V_EVAC else "s")
 
-        for w in range(4, LEAD0):
-            widen_piece(w)
         for k in range(2):
             extra()
         weights_copy("g", "s")
-        tables_c()
         weights_quant("g")
-        for k in range(HEADX):
-            extra()
+        for w in range(4, LEAD0 - LEAD + 4):
+            widen_piece(w)
         vdone = 0
-        for w in range(5, LEAD):
-            x_piece(w)
-            if w - 5 < VLEAD:
+        for w in range(4, LEAD):
+            widen_piece(w + LEAD0 - LEAD)
+            if vdone < VLEAD and vdone // 4 in x_codes:
                 value_piece(vdone)
                 vdone += 1
+            x_piece(w)
+            if w == GATE0:
+                for k in range(LAG):
+                    gate(*units[k])
+            if (w - 4) * HNUM // 4 > (w - 5) * HNUM // 4:
+                extra()
         while vdone < VLEAD:
             value_piece(vdone)
             vdone += 1
-        for k in range(LAG):
-            gate(*units[k])
         hx = 0
         for s in range(len(units)):
             g, q = units[s]
@@ -489,8 +502,10 @@ def tile_decayed_event_risk_f4_kernel(
                     widen_piece(s + LEAD0)
                 if item == "x":
                     x_piece(s + LEAD)
-                if item == "evq" and s >= 4 and s % 4 == 0:
+                if item == "evq" and s >= 4 and s % 4 == 0 and s <= 24:
                     event_quant(s // 4 - 1, 0, OUTCOMES)
+                if item == "evq" and s >= 26 and s % 2 == 0:
+                    event_quant(6 + (s - 26) // 2 % 2, (s - 26) // 4 * HALF, (s - 26) // 4 * HALF + HALF)
                 if item == "value":
                     value_piece(s + VLEAD)
                 if item == "event":
@@ -504,31 +519,30 @@ def tile_decayed_event_risk_f4_kernel(
                         sp_min(i, 0)
                     if s % 8 == SPE:
                         sp_exp(i, 0)
+                if item == "pool" and s == PL0:
+                    pooled(PATIENTS - 1, 0, 0)
+                    pooled(PATIENTS - 1, 0, 1)
+                    sp_min(PATIENTS - 1, 0)
+                if item == "pool" and s == PL1:
+                    sp_exp(PATIENTS - 1, 0)
                 if item == "extra":
-                    while pending and s % 2 == 1:
+                    while pending and (s % 2 == 1 or s > 26):
                         weight_quant(pending.pop(0))
                     if (s * XNUM) // XDEN > hx:
                         hx += 1
                         extra()
-            if s == len(units) - 2:
-                event_quant(g, 0, OUTCOMES // 2)
             if s == MLN:
                 for i in range(MLP):
                     sp_ln(i, 0)
                 nc.scalar.activation(out=warm[:], in_=warm[:], func=ACT.Exp)
                 for i in range(MLP):
                     sp_max(i, 0)
-        while extras:
-            extra()
-        while pending:
-            weight_quant(pending.pop(0))
         last = PATIENTS - 1
-        event_quant(GROUPS - 1, OUTCOMES // 2, OUTCOMES)
-        for h in range(PIECES[last]):
-            for a in range(2):
-                pooled(last, h, a)
-            sp_min(last, h)
-            sp_exp(last, h)
+        event_quant(GROUPS - 1, HALF, OUTCOMES)
+        for a in range(2):
+            pooled(last, 1, a)
+        sp_min(last, 1)
+        sp_exp(last, 1)
         todo = [(i, h) for i in range(MLP, PATIENTS) for h in range(PIECES[i])]
         for i, h in todo:
             sp_ln(i, h)

@@ -22,26 +22,31 @@ SOFTPLUS_CAP = 30.0
 PIECES = (1, 1, 1, 2)
 HALF = OUTCOMES // 2
 XW_BUFS = 4
-LAG = 3
+LAG = 2
 LEAD = 12
-LEAD0 = 12
+LEAD0 = 21
 VLEAD = 6
 PO0 = 0
-PO1 = 2
-SPE = 4
+PO1 = 1
+SPE = 7
 XNUM = 3
 XDEN = 4
 MLN = 99
 MLP = 0
-V_EVAC = (5, 7, 9, 13, 16, 18, 23, 25, 27, 30,)
-ORDER = ("extra", "evq", "widen", "event", "x", "gate", "value", "pool",)
+ORDER = ("gate", "x", "evq", "event", "extra", "value", "widen", "pool",)
 X_MODE = ("v", "x", "x", "x", "x", "x", "x", "x",)
-S_TURN = (4, 6, 7, 8, 9, 10, 11, 12, 13, 14, 15,)
 COMBINE = (1, 2, 3,)
 PL0 = 31
 PL1 = 31
 GATE0 = 8
-HNUM = 3
+HNUM = 4
+BANKS = {"gate":2,"tt":2,"val":2,"m":2}
+WE = ("s", "s",)
+TABC = 5
+TAIL = 1
+G_MIN = (0, 1, 2,)
+V_EVAC = (2, 5, 15, 16, 21, 22, 24, 30,)
+S_TURN = (2, 3, 6, 7, 8, 9, 10, 11, 14,)
 
 
 def tile_decayed_event_risk_f4_kernel(
@@ -55,7 +60,7 @@ def tile_decayed_event_risk_f4_kernel(
         ctx.enter_context(tc.manual_schedule())
 
         def bank(tag, name, shape, dtype=F32):
-            return psum.tile(shape, dtype, name=name, tag=tag, bufs=2)
+            return psum.tile(shape, dtype, name=name, tag=tag, bufs=BANKS[tag])
 
         rows = const.tile([P, 512], BF16, name="rows")
         prows = const.tile([P, P], BF16, name="prows")
@@ -96,12 +101,11 @@ def tile_decayed_event_risk_f4_kernel(
 
         load_x(0)
         nc.sync.dma_start(out=xs_col[:], in_=x_scale.rearrange("a b (p f) -> (a b p) f", f=4))
-        if "x" in X_MODE:
-            nc.sync.dma_start(out=xs_row[:], in_=x_scale.rearrange("a b k -> (a b k)").partition_broadcast(P))
-        load_age(0)
         nc.sync.dma_start(out=w_raw["v"][:], in_=w_value.rearrange("(p j) n -> p j n", j=4))
         nc.sync.dma_start(out=w_raw["g"][:], in_=w_gate.rearrange("(p j) n -> p j n", j=4))
+        nc.sync.dma_start(out=xs_row[:], in_=x_scale.rearrange("a b k -> (a b k)").partition_broadcast(P))
         load_x(1)
+        load_age(0)
         load_x(2)
         load_age(1)
         load_x(3)
@@ -120,7 +124,8 @@ def tile_decayed_event_risk_f4_kernel(
         make_identity(nc, ident_f[:])
         neg_half = const.tile([P, 2], F32, name="neg_half")
         nc.gpsimd.memset(neg_half[:], -0.5)
-
+        neg_one = const.tile([P, 1], F32, name="neg_one")
+        nc.gpsimd.memset(neg_one[:], -1.0)
         mix_cols = const.tile([P, 2, PATIENTS * P], F32, name="mix_cols")
         nc.gpsimd.memset(mix_cols[:], 0.0)
 
@@ -128,18 +133,11 @@ def tile_decayed_event_risk_f4_kernel(
         for t in range(4):
             nc.tensor.transpose(cols_ps[:, t, :], rows[:, t : 512 : 4], ident_b[:])
         cols = const.tile([P, 24, 4], F32, name="cols")
-        nc.vector.tensor_copy(out=cols[:], in_=cols_ps[:, :, 0:24].rearrange("p t c -> p c t"))
+        nc.scalar.copy(out=cols[:], in_=cols_ps[:, :, 0:24].rearrange("p t c -> p c t"))
         prm_ps = bank("m", "prm_ps", [P, P], BF16)
         nc.tensor.transpose(prm_ps[:], prows[:], ident_b[:])
         prm = const.tile([P, 10], F32, name="prm")
-        nc.vector.tensor_copy(out=prm[:], in_=prm_ps[:, 0:10])
-        rate_m2 = const.tile([P, 2], F32, name="rate_m2")
-        nc.vector.tensor_scalar(out=rate_m2[:], in0=prm[:, 0:2], scalar1=-2.0, scalar2=None, op0=ALU.mult)
-        for a in range(2):
-            nc.gpsimd.tensor_copy(
-                out=mix_cols[:, a, 0 : 3 * P + 4 : P + 1], in_=prm[:, 4 + a : 5 + a].to_broadcast([P, PATIENTS])
-            )
-        mix_ratio = const.tile([P, 1], F32, name="mix_ratio")
+        nc.scalar.copy(out=prm[:], in_=prm_ps[:, 0:10])
         rel_c = cols[:, 8:16, :].rearrange("p c t -> p (c t)")
         l0 = const.tile([P, 32], F32, name="l0")
         inv = const.tile([P, 32], F32, name="inv")
@@ -147,40 +145,45 @@ def tile_decayed_event_risk_f4_kernel(
         nc.scalar.activation(out=inv[:], in_=l0[:], func=ACT.Exp, scale=-1.0)
         sev_half = const.tile([P, 32], F32, name="sev_half")
         bias_half = const.tile([P, 4], F32, name="bias_half")
+        rate_m2 = const.tile([P, 2], F32, name="rate_m2")
+        mix_ratio = const.tile([P, 1], F32, name="mix_ratio")
         mask_t = const.tile([P, 4], F32, name="mask_t")
         mask_g = const.tile([P, GROUPS], F32, name="mask_g")
         lnrel = const.tile([P, 32], F32, name="lnrel")
         parts = const.tile([P, 4, 32], BF16, name="parts")
         parts_t = const.tile([P, P], BF16, name="parts_t")
         arg_rhs = const.tile([P, 2, 4, P], BF16, name="arg_rhs")
-        arg_lhs = []
+        arg_lhs = {}
 
         def tables_a():
-            nc.gpsimd.tensor_scalar(
-                out=sev_half[:], in0=cols[:, 16:24, :].rearrange("p c t -> p (c t)"),
-                scalar1=0.5, scalar2=0.0, op0=ALU.mult, op1=ALU.add,
-            )
-            nc.gpsimd.tensor_scalar(
-                out=bias_half[:], in0=prm[:, 6:10], scalar1=0.5, scalar2=0.0, op0=ALU.mult, op1=ALU.add
-            )
-            nc.gpsimd.tensor_copy(out=parts[:, 0, :], in_=cols[:, 0:8, :].rearrange("p c t -> p (c t)"))
             nc.gpsimd.tensor_tensor(out=lnrel[:], in0=inv[:], in1=rel_c, op=ALU.mult)
             nc.gpsimd.tensor_scalar(
                 out=lnrel[:], in0=lnrel[:], scalar1=-1.0, scalar2=0.0, op0=ALU.add, op1=ALU.add
             )
             nc.gpsimd.tensor_tensor(out=lnrel[:], in0=lnrel[:], in1=l0[:], op=ALU.add)
+            nc.gpsimd.tensor_scalar(
+                out=sev_half[:], in0=cols[:, 16:24, :].rearrange("p c t -> p (c t)"),
+                scalar1=0.5, scalar2=0.0, op0=ALU.mult, op1=ALU.add,
+            )
+            nc.gpsimd.tensor_copy(out=parts[:, 0, :], in_=cols[:, 0:8, :].rearrange("p c t -> p (c t)"))
             for s in (1, 2, 3):
                 nc.gpsimd.tensor_copy(out=parts[:, s, :], in_=lnrel[:])
                 if s < 3:
                     nc.gpsimd.tensor_tensor(out=lnrel[:], in0=lnrel[:], in1=parts[:, s, :], op=ALU.subtract)
-            parts_ps = bank("m", "parts_ps", [P, P], BF16)
-            nc.tensor.transpose(parts_ps[:], parts[:].rearrange("p s c -> p (s c)"), ident_b[:])
-            return parts_ps
+            nc.gpsimd.tensor_scalar(
+                out=rate_m2[:], in0=prm[:, 0:2], scalar1=-2.0, scalar2=0.0, op0=ALU.mult, op1=ALU.add
+            )
+            nc.gpsimd.tensor_scalar(
+                out=bias_half[:], in0=prm[:, 6:10], scalar1=0.5, scalar2=0.0, op0=ALU.mult, op1=ALU.add
+            )
+            nc.gpsimd.tensor_tensor(out=mix_ratio[:], in0=prm[:, 4:5], in1=neg_one[:], op=ALU.pow)
+            nc.gpsimd.tensor_tensor(out=mix_ratio[:], in0=mix_ratio[:], in1=prm[:, 5:6], op=ALU.mult)
+            for a in range(2):
+                nc.gpsimd.tensor_copy(
+                    out=mix_cols[:, a, 0 : 3 * P + 4 : P + 1], in_=prm[:, 4 + a : 5 + a].to_broadcast([P, PATIENTS])
+                )
 
-        def tables_b0(parts_ps):
-            if COMBINE:
-                nc.vector.reciprocal(out=mix_ratio[:], in_=prm[:, 4:5])
-                nc.vector.tensor_tensor(out=mix_ratio[:], in0=mix_ratio[:], in1=prm[:, 5:6], op=ALU.mult)
+        def tables_v():
             nc.vector.tensor_reduce(
                 out=mask_t[:], in_=ident_f[:].rearrange("p (q t) -> p t q", t=4), axis=AX.X, op=ALU.add
             )
@@ -190,22 +193,20 @@ def tile_decayed_event_risk_f4_kernel(
             nc.vector.tensor_scalar(
                 out=mask_t[0:32, :], in0=mask_t[0:32, :], scalar1=-1.0, scalar2=None, op0=ALU.mult
             )
-            nc.vector.tensor_copy(out=parts_t[:], in_=parts_ps[:])
 
         def tables_c():
+            parts_ps = bank("m", "parts_ps", [P, P], BF16)
+            nc.tensor.transpose(parts_ps[:], parts[:].rearrange("p s c -> p (s c)"), ident_b[:])
+            nc.scalar.copy(out=parts_t[:], in_=parts_ps[:])
             for t in range(4):
-                nc.vector.tensor_scalar(
-                    out=arg_rhs[:, :, t, :], in0=val[:].rearrange("p (a j) -> p a j", j=P),
-                    scalar1=mask_t[:, t : t + 1], scalar2=None, op0=ALU.mult,
+                nc.scalar.activation(
+                    out=arg_rhs[:, :, t, :], in_=val[:].rearrange("p (a j) -> p a j", j=P),
+                    func=ACT.Copy, scale=mask_t[:, t : t + 1],
                 )
 
-        def tables_b(groups):
-            for g in groups:
-                lhs_g = const.tile([P, P], BF16, name="arg_lhs%d" % g)
-                nc.vector.tensor_scalar(
-                    out=lhs_g[:], in0=parts_t[:], scalar1=mask_g[:, g : g + 1], scalar2=None, op0=ALU.mult
-                )
-                arg_lhs.append(lhs_g)
+        def tables_b(g):
+            arg_lhs[g] = const.tile([P, P], BF16, name="arg_lhs%d" % g)
+            nc.scalar.activation(out=arg_lhs[g][:], in_=parts_t[:], func=ACT.Copy, scale=mask_g[:, g : g + 1])
 
         w_codes, w_scales = {}, {}
 
@@ -391,8 +392,9 @@ def tile_decayed_event_risk_f4_kernel(
             nc.sync.dma_start(out=score[i, j, n], in_=sc[i][:, h, a, :])
 
         def sp_min(i, h):
-            nc.vector.tensor_scalar(
-                out=sp[i][:, h], in0=sc[i][:, h], scalar1=SOFTPLUS_CAP, scalar2=None, op0=ALU.min
+            engine = nc.gpsimd if i in G_MIN else nc.vector
+            engine.tensor_scalar(
+                out=sp[i][:, h], in0=sc[i][:, h], scalar1=SOFTPLUS_CAP, scalar2=0.0, op0=ALU.min, op1=ALU.add
             )
 
         def sp_exp(i, h):
@@ -425,16 +427,17 @@ def tile_decayed_event_risk_f4_kernel(
                         start=(i == 0 and a == 0), stop=(i == PATIENTS - 1 and a == (0 if i in COMBINE else 1)),
                     )
 
+        tables_a()
         for t in range(4):
             x_widen(0, t)
+        tables_v()
         x_turn(0, 0)
         x_turn(0, 1)
+        weights_copy("v", WE[0])
+        weights_copy("g", WE[1])
         x_quant(0)
-        weights_copy("v", "v")
         weights_quant("v")
-        parts_ps = tables_a()
-        tables_b0(parts_ps)
-        tables_c()
+        weights_quant("g")
         extras = []
         for i in range(PATIENTS):
             extras += [("size", i, 0), ("size", i, 1)]
@@ -448,7 +451,7 @@ def tile_decayed_event_risk_f4_kernel(
                 kind, g, a = extras.pop()
                 if kind == "size":
                     size(g, a)
-                    tables_b((2 * g + a,))
+                    tables_b(2 * g + a)
                 else:
                     weight_exp(g, a)
                     if a == 1:
@@ -471,10 +474,6 @@ def tile_decayed_event_risk_f4_kernel(
             if v < len(units):
                 value(v // 4, v % 4, "v" if v in V_EVAC else "s")
 
-        for k in range(2):
-            extra()
-        weights_copy("g", "s")
-        weights_quant("g")
         for w in range(4, LEAD0 - LEAD + 4):
             widen_piece(w)
         vdone = 0
@@ -487,8 +486,11 @@ def tile_decayed_event_risk_f4_kernel(
             if w == GATE0:
                 for k in range(LAG):
                     gate(*units[k])
-            if (w - 4) * HNUM // 4 > (w - 5) * HNUM // 4:
-                extra()
+            if w == TABC:
+                tables_c()
+            if w >= TABC:
+                for k in range((w - TABC + 1) * HNUM // 4 - (w - TABC) * HNUM // 4):
+                    extra()
         while vdone < VLEAD:
             value_piece(vdone)
             vdone += 1
@@ -523,7 +525,7 @@ def tile_decayed_event_risk_f4_kernel(
                     pooled(PATIENTS - 1, 0, 0)
                     pooled(PATIENTS - 1, 0, 1)
                     sp_min(PATIENTS - 1, 0)
-                if item == "pool" and s == PL1:
+                if item == "pool" and s == PL1 and TAIL == 0:
                     sp_exp(PATIENTS - 1, 0)
                 if item == "extra":
                     while pending and (s % 2 == 1 or s > 26):
@@ -539,13 +541,20 @@ def tile_decayed_event_risk_f4_kernel(
                     sp_max(i, 0)
         last = PATIENTS - 1
         event_quant(GROUPS - 1, HALF, OUTCOMES)
+        if TAIL == 1:
+            for i in range(last):
+                sp_ln(i, 0)
+            nc.scalar.activation(out=warm[:], in_=warm[:], func=ACT.Exp)
         for a in range(2):
             pooled(last, 1, a)
         sp_min(last, 1)
+        if TAIL == 1:
+            sp_exp(last, 0)
         sp_exp(last, 1)
         todo = [(i, h) for i in range(MLP, PATIENTS) for h in range(PIECES[i])]
         for i, h in todo:
-            sp_ln(i, h)
+            if TAIL == 0 or i == last:
+                sp_ln(i, h)
         for i in range(MLP):
             sp_sum(i, 0)
         for i, h in todo:

from contextlib import ExitStack

import concourse.mybir as mybir
from concourse.masks import make_identity

PATIENTS, EVENTS, FEATURES, OUTCOMES, RATES = 4, 1024, 512, 512, 256
FLOPS = 2 * PATIENTS * EVENTS * FEATURES * OUTCOMES * 2 + 2 * PATIENTS * RATES * EVENTS * OUTCOMES

P = 128
F32 = mybir.dt.float32
BF16 = mybir.dt.bfloat16
U32 = mybir.dt.uint32
U8 = mybir.dt.uint8
E4M3 = mybir.dt.float8_e4m3fn
E4M3X4 = mybir.dt.float8_e4m3fn_x4
ALU = mybir.AluOpType
ACT = mybir.ActivationFunctionType
AX = mybir.AxisListType

GROUPS = PATIENTS * EVENTS // 512
SOFTPLUS_CAP = 30.0
PIECES = (1, 1, 1, 2)
HALF = OUTCOMES // 2
XW_BUFS = 4
LAG = 2
LEAD = 12
LEAD0 = 21
VLEAD = 6
PO0 = 0
PO1 = 1
SPE = 7
XNUM = 3
XDEN = 4
MLN = 99
MLP = 0
ORDER = ("gate", "x", "evq", "event", "extra", "value", "widen", "pool",)
X_MODE = ("v", "x", "x", "x", "x", "x", "x", "x",)
COMBINE = (1, 2, 3,)
PL0 = 31
PL1 = 31
GATE0 = 8
HNUM = 4
BANKS = {"gate":2,"tt":2,"val":2,"m":2}
WE = ("s", "s",)
TABC = 5
TAIL = 1
G_MIN = (0, 1, 2,)
V_EVAC = (2, 5, 15, 16, 21, 22, 24, 30,)
S_TURN = (2, 3, 6, 7, 8, 9, 10, 11, 14,)


def tile_decayed_event_risk_f4_kernel(
    tc, x_bytes, x_scale, w_value, w_gate, gate_bias, severity, reliability, age, rate, amp, base, mix, score, risk
):
    nc = tc.nc
    with ExitStack() as ctx:
        const = ctx.enter_context(tc.tile_pool(name="const", bufs=1))
        work = ctx.enter_context(tc.tile_pool(name="work", bufs=2))
        psum = ctx.enter_context(tc.psum_pool(name="psum", bufs=2))
        ctx.enter_context(tc.manual_schedule())

        def bank(tag, name, shape, dtype=F32):
            return psum.tile(shape, dtype, name=name, tag=tag, bufs=BANKS[tag])

        rows = const.tile([P, 512], BF16, name="rows")
        prows = const.tile([P, P], BF16, name="prows")
        val = const.tile([P, RATES], BF16, name="val")
        nc.vector.memset(rows[:], 0.0)
        nc.vector.memset(prows[:], 0.0)
        nc.vector.memset(val[:], 1.0)
        warm = const.tile([P, 1], F32, name="warm")
        nc.vector.memset(warm[:], 1.0)

        x_view = x_bytes.rearrange("i (g p t) k -> (i g) p (t k)", g=2, p=P, t=4)
        xb = []
        for g in range(GROUPS):
            xb_g = const.tile([P, 2048], U8, name="xb%d" % g, align_bytes=64)
            xb.append(xb_g)
        age_b = const.tile([P, PATIENTS, EVENTS], BF16, name="age_b")
        w_raw = {}
        for key in ("g", "v"):
            raw = const.tile([P, 4, OUTCOMES], BF16, name="w_raw_" + key)
            w_raw[key] = raw
        xs_col = const.tile([P, 4], F32, name="xs_col")
        xs_row = const.tile([P, FEATURES], F32, name="xs_row")
        base_b = const.tile([P, OUTCOMES], BF16, name="base_b")
        nc.scalar.dma_start(out=rows[8:16, :], in_=reliability.rearrange("i (g q) -> (i g) q", g=2))
        nc.scalar.dma_start(out=rows[0:8, :], in_=age.rearrange("i (g q) -> (i g) q", g=2))
        nc.scalar.dma_start(out=prows[0:2, :], in_=rate.rearrange("(a b) -> a b", b=P))
        nc.scalar.dma_start(out=rows[16:24, :], in_=severity.rearrange("i (g q) -> (i g) q", g=2))
        nc.scalar.dma_start(out=prows[2:4, :], in_=amp.rearrange("(a b) -> a b", b=P))
        nc.scalar.dma_start(out=prows[4:6, :], in_=mix.rearrange("(a b) -> a b", b=P))
        nc.scalar.dma_start(out=prows[6:10, :], in_=gate_bias.rearrange("(a b) -> a b", b=P))
        nc.scalar.dma_start(out=val[0:32, :], in_=rate.partition_broadcast(32))

        def load_x(g):
            nc.sync.dma_start(out=xb[g][:], in_=x_view[g])

        def load_age(i):
            nc.sync.dma_start(out=age_b[:, i, :], in_=age[i].partition_broadcast(P))

        load_x(0)
        nc.sync.dma_start(out=xs_col[:], in_=x_scale.rearrange("a b (p f) -> (a b p) f", f=4))
        nc.sync.dma_start(out=w_raw["v"][:], in_=w_value.rearrange("(p j) n -> p j n", j=4))
        nc.sync.dma_start(out=w_raw["g"][:], in_=w_gate.rearrange("(p j) n -> p j n", j=4))
        nc.sync.dma_start(out=xs_row[:], in_=x_scale.rearrange("a b k -> (a b k)").partition_broadcast(P))
        load_x(1)
        load_age(0)
        load_x(2)
        load_age(1)
        load_x(3)
        load_x(4)
        load_age(2)
        load_x(5)
        load_age(3)
        nc.sync.dma_start(out=base_b[:], in_=base.partition_broadcast(P))
        load_x(6)
        load_x(7)

        nc.scalar.activation(out=warm[:], in_=warm[:], func=ACT.Ln)
        ident_b = const.tile([P, P], BF16, name="ident_b")
        make_identity(nc, ident_b[:])
        ident_f = const.tile([P, P], F32, name="ident_f")
        make_identity(nc, ident_f[:])
        neg_half = const.tile([P, 2], F32, name="neg_half")
        nc.gpsimd.memset(neg_half[:], -0.5)
        neg_one = const.tile([P, 1], F32, name="neg_one")
        nc.gpsimd.memset(neg_one[:], -1.0)
        mix_cols = const.tile([P, 2, PATIENTS * P], F32, name="mix_cols")
        nc.gpsimd.memset(mix_cols[:], 0.0)

        cols_ps = bank("m", "cols_ps", [P, 4, P], BF16)
        for t in range(4):
            nc.tensor.transpose(cols_ps[:, t, :], rows[:, t : 512 : 4], ident_b[:])
        cols = const.tile([P, 24, 4], F32, name="cols")
        nc.scalar.copy(out=cols[:], in_=cols_ps[:, :, 0:24].rearrange("p t c -> p c t"))
        prm_ps = bank("m", "prm_ps", [P, P], BF16)
        nc.tensor.transpose(prm_ps[:], prows[:], ident_b[:])
        prm = const.tile([P, 10], F32, name="prm")
        nc.scalar.copy(out=prm[:], in_=prm_ps[:, 0:10])
        rel_c = cols[:, 8:16, :].rearrange("p c t -> p (c t)")
        l0 = const.tile([P, 32], F32, name="l0")
        inv = const.tile([P, 32], F32, name="inv")
        nc.scalar.activation(out=l0[:], in_=rel_c, func=ACT.Ln)
        nc.scalar.activation(out=inv[:], in_=l0[:], func=ACT.Exp, scale=-1.0)
        sev_half = const.tile([P, 32], F32, name="sev_half")
        bias_half = const.tile([P, 4], F32, name="bias_half")
        rate_m2 = const.tile([P, 2], F32, name="rate_m2")
        mix_ratio = const.tile([P, 1], F32, name="mix_ratio")
        mask_t = const.tile([P, 4], F32, name="mask_t")
        mask_g = const.tile([P, GROUPS], F32, name="mask_g")
        lnrel = const.tile([P, 32], F32, name="lnrel")
        parts = const.tile([P, 4, 32], BF16, name="parts")
        parts_t = const.tile([P, P], BF16, name="parts_t")
        arg_rhs = const.tile([P, 2, 4, P], BF16, name="arg_rhs")
        arg_lhs = {}

        def tables_a():
            nc.gpsimd.tensor_tensor(out=lnrel[:], in0=inv[:], in1=rel_c, op=ALU.mult)
            nc.gpsimd.tensor_scalar(
                out=lnrel[:], in0=lnrel[:], scalar1=-1.0, scalar2=0.0, op0=ALU.add, op1=ALU.add
            )
            nc.gpsimd.tensor_tensor(out=lnrel[:], in0=lnrel[:], in1=l0[:], op=ALU.add)
            nc.gpsimd.tensor_scalar(
                out=sev_half[:], in0=cols[:, 16:24, :].rearrange("p c t -> p (c t)"),
                scalar1=0.5, scalar2=0.0, op0=ALU.mult, op1=ALU.add,
            )
            nc.gpsimd.tensor_copy(out=parts[:, 0, :], in_=cols[:, 0:8, :].rearrange("p c t -> p (c t)"))
            for s in (1, 2, 3):
                nc.gpsimd.tensor_copy(out=parts[:, s, :], in_=lnrel[:])
                if s < 3:
                    nc.gpsimd.tensor_tensor(out=lnrel[:], in0=lnrel[:], in1=parts[:, s, :], op=ALU.subtract)
            nc.gpsimd.tensor_scalar(
                out=rate_m2[:], in0=prm[:, 0:2], scalar1=-2.0, scalar2=0.0, op0=ALU.mult, op1=ALU.add
            )
            nc.gpsimd.tensor_scalar(
                out=bias_half[:], in0=prm[:, 6:10], scalar1=0.5, scalar2=0.0, op0=ALU.mult, op1=ALU.add
            )
            nc.gpsimd.tensor_tensor(out=mix_ratio[:], in0=prm[:, 4:5], in1=neg_one[:], op=ALU.pow)
            nc.gpsimd.tensor_tensor(out=mix_ratio[:], in0=mix_ratio[:], in1=prm[:, 5:6], op=ALU.mult)
            for a in range(2):
                nc.gpsimd.tensor_copy(
                    out=mix_cols[:, a, 0 : 3 * P + 4 : P + 1], in_=prm[:, 4 + a : 5 + a].to_broadcast([P, PATIENTS])
                )

        def tables_v():
            nc.vector.tensor_reduce(
                out=mask_t[:], in_=ident_f[:].rearrange("p (q t) -> p t q", t=4), axis=AX.X, op=ALU.add
            )
            nc.vector.tensor_reduce(
                out=mask_g[:], in_=ident_f[:].rearrange("p (s g t) -> p g s t", s=4, t=4), axis=AX.XY, op=ALU.add
            )
            nc.vector.tensor_scalar(
                out=mask_t[0:32, :], in0=mask_t[0:32, :], scalar1=-1.0, scalar2=None, op0=ALU.mult
            )

        def tables_c():
            parts_ps = bank("m", "parts_ps", [P, P], BF16)
            nc.tensor.transpose(parts_ps[:], parts[:].rearrange("p s c -> p (s c)"), ident_b[:])
            nc.scalar.copy(out=parts_t[:], in_=parts_ps[:])
            for t in range(4):
                nc.scalar.activation(
                    out=arg_rhs[:, :, t, :], in_=val[:].rearrange("p (a j) -> p a j", j=P),
                    func=ACT.Copy, scale=mask_t[:, t : t + 1],
                )

        def tables_b(g):
            arg_lhs[g] = const.tile([P, P], BF16, name="arg_lhs%d" % g)
            nc.scalar.activation(out=arg_lhs[g][:], in_=parts_t[:], func=ACT.Copy, scale=mask_g[:, g : g + 1])

        w_codes, w_scales = {}, {}

        def weights_copy(key, engine):
            grouped = work.tile([P, OUTCOMES, 4], BF16, name="w_grouped_" + key, tag="w_grouped", bufs=2, align_bytes=64)
            w_codes[key] = grouped
            if engine == "v":
                nc.vector.tensor_copy(out=grouped[:], in_=w_raw[key][:].rearrange("p j n -> p n j"))
            else:
                nc.scalar.copy(out=grouped[:], in_=w_raw[key][:].rearrange("p j n -> p n j"))

        def weights_quant(key):
            grouped = w_codes[key]
            codes = const.tile([P, OUTCOMES], U32, name="w_codes_" + key, align_bytes=64)
            scales = const.tile([P, OUTCOMES], U8, name="w_scales_" + key, align_bytes=64)
            nc.vector.quantize_mx(
                out=codes[:].bitcast(E4M3X4), scales=scales[:], in_=grouped[:].rearrange("p n j -> p (n j)")
            )
            w_codes[key], w_scales[key] = codes, scales

        xw, xi, x_codes, x_scales = {}, {}, {}, {}

        def x_widen(g, t):
            if t == 0:
                xw[g] = work.tile([P, 2048], BF16, name="xw%d" % g, tag="xw", bufs=XW_BUFS)
            c = slice(FEATURES * t, FEATURES * (t + 1))
            src = xb[g][:, c].bitcast(E4M3)
            mode = X_MODE[g]
            if mode == "x":
                nc.vector.tensor_tensor(out=xw[g][:, c], in0=src, in1=xs_row[:], op=ALU.mult)
            elif mode == "v":
                nc.vector.tensor_copy(out=xw[g][:, c], in_=src)
            elif mode == "s":
                nc.scalar.copy(out=xw[g][:, c], in_=src)
            else:
                nc.gpsimd.tensor_copy(out=xw[g][:, c], in_=src)

        def x_turn(g, h):
            if h == 0:
                xi[g] = work.tile([P, 512, 4], BF16, name="xi%d" % g, tag="xi", bufs=2, align_bytes=64)
            words = xw[g][:].bitcast(F32)
            turned = bank("m", "xt%d_%d" % (g, h), [P, 2, 2, P])
            for t in range(2):
                for u in range(2):
                    c0 = 256 * (2 * h + t)
                    nc.tensor.transpose(turned[:, u, t, :], words[:, c0 + u : c0 + 256 : 2], ident_f[:])
            if X_MODE[g] == "x":
                words_out = xi[g][:].rearrange("p n f -> p (n f)").bitcast(F32)[:, 512 * h : 512 * (h + 1)]
                words_out = words_out.rearrange("p (n u) -> p n u", u=2)
                words_in = turned[:].rearrange("p u t r -> p (t r) u")
                if 2 * g + h in S_TURN:
                    nc.scalar.copy(out=words_out, in_=words_in)
                else:
                    nc.vector.tensor_copy(out=words_out, in_=words_in)
                return
            pairs = turned[:].rearrange("p u t r -> p (u t r)").bitcast(BF16)
            nc.vector.tensor_tensor(
                out=xi[g][:, 256 * h : 256 * (h + 1), :].rearrange("p n (u e) -> p n u e", u=2),
                in0=pairs.rearrange("p (u n e) -> p n u e", u=2, e=2),
                in1=xs_col[:].rearrange("p (o u e) -> p o u e", o=1, u=2).to_broadcast([P, 256, 2, 2]),
                op=ALU.mult,
            )

        def x_quant(g):
            codes = const.tile([P, 512], U32, name="x_codes%d" % g, align_bytes=64)
            scales = const.tile([P, 512], U8, name="x_scales%d" % g, align_bytes=64)
            nc.vector.quantize_mx(
                out=codes[:].bitcast(E4M3X4), scales=scales[:], in_=xi[g][:].rearrange("p n f -> p (n f)")
            )
            x_codes[g], x_scales[g] = codes, scales

        sum_sq = const.tile([P, PATIENTS, 2], F32, name="sum_sq")
        amp_over_size = const.tile([P, PATIENTS, 2], F32, name="amp_over_size")

        def size(i, a):
            junk = work.tile([P, EVENTS], BF16, name="junk%d_%d" % (i, a), tag="junk", bufs=2)
            nc.scalar.activation(
                out=junk[:], in_=age_b[:, i, :], func=ACT.Exp, scale=rate_m2[:, a : a + 1],
                accum_out=sum_sq[:, i, a : a + 1],
            )
            if a == 1:
                nc.gpsimd.tensor_tensor(out=amp_over_size[:, i, :], in0=sum_sq[:, i, :], in1=neg_half[:], op=ALU.pow)
                nc.gpsimd.tensor_tensor(
                    out=amp_over_size[:, i, :], in0=amp_over_size[:, i, :], in1=prm[:, 2:4], op=ALU.mult
                )

        wt, wt_codes, wt_scales = {}, {}, {}

        def weight_exp(g, a):
            if a == 0:
                wt[g] = work.tile([P, RATES, 4], BF16, name="wt%d" % g, tag="wt", bufs=4, align_bytes=64)
            arg = bank("m", "arg%d_%d" % (g, a), [P, 4, P])
            nc.tensor.matmul(
                arg[:].rearrange("p t j -> p (t j)"), lhsT=arg_lhs[g][:],
                rhs=arg_rhs[:, a].rearrange("p t j -> p (t j)"), start=True, stop=True,
            )
            nc.scalar.activation(
                out=wt[g][:, P * a : P * (a + 1), :], in_=arg[:].rearrange("p t j -> p j t"), func=ACT.Exp
            )

        def weight_quant(g):
            codes = const.tile([P, RATES], U32, name="wt_codes%d" % g, align_bytes=64)
            scales = const.tile([P, RATES], U8, name="wt_scales%d" % g, align_bytes=64)
            nc.vector.quantize_mx(
                out=codes[:].bitcast(E4M3X4), scales=scales[:], in_=wt[g][:].rearrange("p j t -> p (j t)")
            )
            wt_codes[g], wt_scales[g] = codes, scales

        val_sb, th, ev, ev_codes, ev_scales = {}, {}, {}, {}, {}

        def value(g, t, engine):
            if t == 0:
                val_sb[g] = work.tile([P, 4, OUTCOMES], F32, name="val_sb%d" % g, tag="val_sb", bufs=3)
            c = slice(P * t, P * (t + 1))
            vb = bank("val", "val%d_%d" % (g, t), [P, OUTCOMES])
            nc.tensor.matmul_mx(
                out=vb[:], lhsT=x_codes[g][:, c].bitcast(E4M3X4), lhsT_scale=x_scales[g][:, c],
                rhs=w_codes["v"][:].bitcast(E4M3X4), rhs_scale=w_scales["v"][:], start=True, stop=True,
            )
            sev = sev_half[:, 4 * g + t : 4 * g + t + 1]
            if engine == "s":
                nc.scalar.activation(out=val_sb[g][:, t, :], in_=vb[:], func=ACT.Copy, scale=sev)
            else:
                nc.vector.tensor_scalar(out=val_sb[g][:, t, :], in0=vb[:], scalar1=sev, scalar2=None, op0=ALU.mult)

        def gate(g, q):
            n = slice(P * q, P * (q + 1))
            gb = bank("gate", "gate%d_%d" % (g, q), [P, 512])
            nc.tensor.matmul_mx(
                out=gb[:], lhsT=w_codes["g"][:, n].bitcast(E4M3X4), lhsT_scale=w_scales["g"][:, n],
                rhs=x_codes[g][:].bitcast(E4M3X4), rhs_scale=x_scales[g][:], start=True, stop=True,
            )
            th[g, q] = work.tile([P, 512], F32, name="th%d_%d" % (g, q), tag="th", bufs=4)
            nc.scalar.activation(out=th[g, q][:], in_=gb[:], func=ACT.Tanh, scale=0.5, bias=bias_half[:, q : q + 1])

        def event(g, q):
            if q == 0:
                ev[g] = work.tile([P, OUTCOMES, 4], BF16, name="ev%d" % g, tag="ev", bufs=3, align_bytes=64)
            n = slice(P * q, P * (q + 1))
            tt = bank("tt", "tt%d_%d" % (g, q), [P, 4, P])
            for t in range(4):
                nc.tensor.transpose(tt[:, t, :], th[g, q][:, P * t : P * (t + 1)], ident_f[:])
            nc.vector.scalar_tensor_tensor(
                out=ev[g][:, n, :], in0=tt[:].rearrange("p t n -> p n t"), scalar=1.0,
                in1=val_sb[g][:, :, n].rearrange("p t n -> p n t"), op0=ALU.add, op1=ALU.mult,
            )

        def event_quant(g, c0, c1):
            if c0 == 0:
                ev_codes[g] = work.tile(
                    [P, OUTCOMES], U32, name="ev_codes%d" % g, tag="ev_codes", bufs=4, align_bytes=64
                )
                ev_scales[g] = work.tile(
                    [P, OUTCOMES], U8, name="ev_scales%d" % g, tag="ev_scales", bufs=4, align_bytes=64
                )
            nc.vector.quantize_mx(
                out=ev_codes[g][:, c0:c1].bitcast(E4M3X4), scales=ev_scales[g][:, c0:c1],
                in_=ev[g][:, c0:c1, :].rearrange("p n t -> p (n t)"),
            )

        sc, sp = {}, {}
        for i in range(PATIENTS):
            shape = [P, PIECES[i], 2, OUTCOMES // PIECES[i]]
            sc[i] = const.tile(shape, F32, name="sc%d" % i)
            sp[i] = const.tile(shape, F32, name="sp%d" % i)

        def pooled(i, h, a):
            width = OUTCOMES // PIECES[i]
            j = slice(P * a, P * (a + 1))
            n = slice(width * h, width * (h + 1))
            pb = bank("m", "pool%d_%d_%d" % (i, a, h), [P, width])
            for k in range(2):
                g = 2 * i + k
                nc.tensor.matmul_mx(
                    out=pb[:], lhsT=wt_codes[g][:, j].bitcast(E4M3X4), lhsT_scale=wt_scales[g][:, j],
                    rhs=ev_codes[g][:, n].bitcast(E4M3X4), rhs_scale=ev_scales[g][:, n],
                    start=(k == 0), stop=(k == 1),
                )
            nc.vector.scalar_tensor_tensor(
                out=sc[i][:, h, a, :], in0=pb[:], scalar=amp_over_size[:, i, a : a + 1],
                in1=base_b[:, n], op0=ALU.mult, op1=ALU.add,
            )
            nc.sync.dma_start(out=score[i, j, n], in_=sc[i][:, h, a, :])

        def sp_min(i, h):
            engine = nc.gpsimd if i in G_MIN else nc.vector
            engine.tensor_scalar(
                out=sp[i][:, h], in0=sc[i][:, h], scalar1=SOFTPLUS_CAP, scalar2=0.0, op0=ALU.min, op1=ALU.add
            )

        def sp_exp(i, h):
            nc.scalar.activation(out=sp[i][:, h], in_=sp[i][:, h], func=ACT.Exp)

        def sp_ln(i, h):
            nc.scalar.activation(out=sp[i][:, h], in_=sp[i][:, h], func=ACT.Ln, bias=1.0)

        def sp_max(i, h):
            nc.vector.tensor_tensor(out=sp[i][:, h], in0=sp[i][:, h], in1=sc[i][:, h], op=ALU.max)
            if i in COMBINE:
                nc.vector.scalar_tensor_tensor(
                    out=sp[i][:, h, 0, :], in0=sp[i][:, h, 1, :], scalar=mix_ratio[:, 0:1],
                    in1=sp[i][:, h, 0, :], op0=ALU.mult, op1=ALU.add,
                )

        haz = {}

        def sp_sum(i, h):
            width = OUTCOMES // PIECES[i]
            for b in range(2):
                if PIECES[i] == 2 and b != h:
                    continue
                if b not in haz:
                    haz[b] = bank("m", "haz%d" % b, [P, HALF])
                n0 = HALF * b - width * h
                for a in range(1 if i in COMBINE else 2):
                    nc.tensor.matmul(
                        haz[b][:], lhsT=mix_cols[:, a, P * i : P * (i + 1)], rhs=sp[i][:, h, a, n0 : n0 + HALF],
                        start=(i == 0 and a == 0), stop=(i == PATIENTS - 1 and a == (0 if i in COMBINE else 1)),
                    )

        tables_a()
        for t in range(4):
            x_widen(0, t)
        tables_v()
        x_turn(0, 0)
        x_turn(0, 1)
        weights_copy("v", WE[0])
        weights_copy("g", WE[1])
        x_quant(0)
        weights_quant("v")
        weights_quant("g")
        extras = []
        for i in range(PATIENTS):
            extras += [("size", i, 0), ("size", i, 1)]
            for g in (2 * i, 2 * i + 1):
                extras += [("exp", g, 0), ("exp", g, 1)]
        extras = extras[::-1]
        pending = []

        def extra():
            if extras:
                kind, g, a = extras.pop()
                if kind == "size":
                    size(g, a)
                    tables_b(2 * g + a)
                else:
                    weight_exp(g, a)
                    if a == 1:
                        pending.append(g)

        def widen_piece(w):
            if 4 <= w < 4 * GROUPS:
                x_widen(w // 4, w % 4)

        def x_piece(w):
            if w % 2 == 0 and 4 < w <= 4 * GROUPS:
                x_turn((w - 1) // 4, (w - 1) % 4 // 2)
            if w % 4 == 1 and 5 < w <= 4 * GROUPS + 1:
                x_quant(w // 4 - 1)

        units = [(g, q) for g in range(GROUPS - 2) for q in range(4)]
        units += [(g, 2 * h + k) for h in range(2) for g in (GROUPS - 2, GROUPS - 1) for k in range(2)]

        def value_piece(v):
            if v < len(units):
                value(v // 4, v % 4, "v" if v in V_EVAC else "s")

        for w in range(4, LEAD0 - LEAD + 4):
            widen_piece(w)
        vdone = 0
        for w in range(4, LEAD):
            widen_piece(w + LEAD0 - LEAD)
            if vdone < VLEAD and vdone // 4 in x_codes:
                value_piece(vdone)
                vdone += 1
            x_piece(w)
            if w == GATE0:
                for k in range(LAG):
                    gate(*units[k])
            if w == TABC:
                tables_c()
            if w >= TABC:
                for k in range((w - TABC + 1) * HNUM // 4 - (w - TABC) * HNUM // 4):
                    extra()
        while vdone < VLEAD:
            value_piece(vdone)
            vdone += 1
        hx = 0
        for s in range(len(units)):
            g, q = units[s]
            for item in ORDER:
                if item == "gate" and s + LAG < len(units):
                    gate(*units[s + LAG])
                if item == "widen":
                    widen_piece(s + LEAD0)
                if item == "x":
                    x_piece(s + LEAD)
                if item == "evq" and s >= 4 and s % 4 == 0 and s <= 24:
                    event_quant(s // 4 - 1, 0, OUTCOMES)
                if item == "evq" and s >= 26 and s % 2 == 0:
                    event_quant(6 + (s - 26) // 2 % 2, (s - 26) // 4 * HALF, (s - 26) // 4 * HALF + HALF)
                if item == "value":
                    value_piece(s + VLEAD)
                if item == "event":
                    event(g, q)
                if item == "pool" and s >= 8:
                    i = s // 8 - 1
                    if s % 8 == PO0:
                        pooled(i, 0, 0)
                    if s % 8 == PO1:
                        pooled(i, 0, 1)
                        sp_min(i, 0)
                    if s % 8 == SPE:
                        sp_exp(i, 0)
                if item == "pool" and s == PL0:
                    pooled(PATIENTS - 1, 0, 0)
                    pooled(PATIENTS - 1, 0, 1)
                    sp_min(PATIENTS - 1, 0)
                if item == "pool" and s == PL1 and TAIL == 0:
                    sp_exp(PATIENTS - 1, 0)
                if item == "extra":
                    while pending and (s % 2 == 1 or s > 26):
                        weight_quant(pending.pop(0))
                    if (s * XNUM) // XDEN > hx:
                        hx += 1
                        extra()
            if s == MLN:
                for i in range(MLP):
                    sp_ln(i, 0)
                nc.scalar.activation(out=warm[:], in_=warm[:], func=ACT.Exp)
                for i in range(MLP):
                    sp_max(i, 0)
        last = PATIENTS - 1
        event_quant(GROUPS - 1, HALF, OUTCOMES)
        if TAIL == 1:
            for i in range(last):
                sp_ln(i, 0)
            nc.scalar.activation(out=warm[:], in_=warm[:], func=ACT.Exp)
        for a in range(2):
            pooled(last, 1, a)
        sp_min(last, 1)
        if TAIL == 1:
            sp_exp(last, 0)
        sp_exp(last, 1)
        todo = [(i, h) for i in range(MLP, PATIENTS) for h in range(PIECES[i])]
        for i, h in todo:
            if TAIL == 0 or i == last:
                sp_ln(i, h)
        for i in range(MLP):
            sp_sum(i, 0)
        for i, h in todo:
            sp_max(i, h)
            sp_sum(i, h)
        nc.scalar.activation(out=warm[:], in_=warm[:], func=ACT.Exp)
        for b in range(2):
            n = slice(HALF * b, HALF * (b + 1))
            risk_sb = const.tile([PATIENTS, HALF], F32, name="risk_sb%d" % b)
            nc.scalar.activation(out=risk_sb[:], in_=haz[b][0:PATIENTS, :], func=ACT.Exp, scale=-1.0)
            nc.vector.tensor_scalar(
                out=risk_sb[:], in0=risk_sb[:], scalar1=-1.0, scalar2=1.0, op0=ALU.mult, op1=ALU.add
            )
            nc.sync.dma_start(out=risk[:, n], in_=risk_sb[:])
